import numpy as np
import ml_dtypes


def mxq(x, axis, fmt="e4m3"):
    dtype, down = {"e4m3": (ml_dtypes.float8_e4m3fn, 7), "e5m2": (ml_dtypes.float8_e5m2, 14)}[fmt]
    v = np.moveaxis(np.asarray(x, np.float32).astype(ml_dtypes.bfloat16).astype(np.float64), axis, -1)
    blocks = v.reshape(v.shape[:-1] + (-1, 32))
    amax = np.abs(blocks).max(-1, keepdims=True)
    byte = np.maximum(np.where(amax > 0, np.frexp(amax)[1] - 1 + 127, 0) - down, 1)
    scale = np.exp2(byte - 127.0)
    codes = (blocks / scale).astype(np.float32).astype(dtype).astype(np.float64)
    return np.moveaxis((codes * scale).reshape(v.shape), -1, axis)


WIDE = False


def mx_kscale(k):
    if not WIDE:
        return np.ones(k)
    levels = np.array([10, -10, 5, -5, 0])
    if k % 512:
        return np.exp2(np.random.permutation(np.resize(levels, k // 32))).repeat(32)
    a = np.empty((k // 512, 16))
    for p in range(k // 512):
        a[p, :8] = np.random.permutation(np.resize(levels, 8))
        for g in range(8):
            far = levels[np.abs(levels - a[p, g]) >= 10]
            a[p, g + 8] = far[np.random.randint(len(far))]
    return np.exp2(a.ravel()).repeat(32)


def f64(x):
    return np.asarray(x).astype(np.float64)


def striped(idx):
    return np.tile(idx.reshape(-1, 16).T, (8, 1)).astype(np.uint16)


def unstriped(offs):
    return offs[:16].T.reshape(-1).astype(np.int64)


E2M1 = np.array([0.0, 0.5, 1.0, 1.5, 2.0, 3.0, 4.0, 6.0, -0.0, -0.5, -1.0, -1.5, -2.0, -3.0, -4.0, -6.0])


def pack_weight(w, fmt):
    k, n = w.shape
    w = f64(np.asarray(w, np.float32).astype(ml_dtypes.bfloat16)).reshape(k // 32, 32, n)
    amax = np.abs(w).max(1)
    if fmt == "e4m3":
        byte = np.frexp(amax)[1] - 1 + 127 - 7
    else:
        mant, ex = np.frexp(amax / 6.0)
        byte = np.where(mant > 0.5, ex, ex - 1) + 127
    byte = np.clip(np.where(amax > 0, byte, 1), 1, 254)
    scaled = (w * np.exp2(127.0 - byte)[:, None, :]).reshape(k, n).astype(np.float32)
    by_word = np.ascontiguousarray(scaled.reshape(k // 512, 128, 4, n).transpose(0, 1, 3, 2))
    if fmt == "e4m3":
        words = by_word.astype(ml_dtypes.float8_e4m3fn).view(np.uint8)
    else:
        c = by_word.astype(ml_dtypes.float4_e2m1fn).view(np.uint8) & 0xF
        words = (c[..., 0::2] | (c[..., 1::2] << 4)).reshape(k // 512, 128, 2 * n)
    return np.ascontiguousarray(words), np.ascontiguousarray(byte.astype(np.uint8).reshape(k // 512, 16, n))


def unpack_weight(words, scales, fmt):
    g, _, n = scales.shape
    words = np.ascontiguousarray(words).reshape(g, 128, n, -1)
    if fmt == "e4m3":
        vals = words.view(ml_dtypes.float8_e4m3fn).astype(np.float64)
    else:
        nib = np.empty((g, 128, n, 4), np.uint8)
        nib[..., 0::2] = words & 0xF
        nib[..., 1::2] = words >> 4
        vals = E2M1[nib]
    vals = vals * np.repeat(np.exp2(scales.astype(np.float64) - 127.0), 8, axis=1)[..., None]
    return vals.transpose(0, 1, 3, 2).reshape(g * 512, n)


def gelu(v):
    return 0.5 * v * (1.0 + np.tanh(np.sqrt(2.0 / np.pi) * (v + 0.044715 * v**3)))


K, K2, H, N, T, S, T2, P = 1024, 512, 1024, 512, 4096, 1024, 2048, 512

def setup_inputs():
    n = np.random.standard_normal
    s = mx_kscale(K)[:, None]
    s2 = mx_kscale(K2)[:, None]
    u = mx_kscale(H)[:, None]
    d = {}
    d["tab_words"], d["tab_scales"] = pack_weight(n((K, T)) * s, "e4m3")
    d["offs"] = striped(np.random.permutation(T)[:S])
    d["tab2_words"], d["tab2_scales"] = pack_weight(n((K2, T2)) * s2, "e4m3")
    d["offs2"] = striped(np.random.permutation(T2)[:P])
    d["pos1"] = striped(np.random.permutation(S)[:P])
    d["w1"] = (n((K, H)) / K ** 0.5 / s * u.T).astype(np.float32)
    d["base"] = (0.7 * n((H, S)) * u).astype(np.float32)
    d["w2_words"], d["w2_scales"] = pack_weight(2.5 * n((K2, H)) / K2 ** 0.5 / s2, "e4m3")
    d["wgs"] = np.exp(0.3 * n((128, P))).astype(np.float32)
    d["w4_words"], d["w4_scales"] = pack_weight(0.29 * n((H, N)) / H ** 0.5 / u, "e2m1")
    d["am"] = np.random.uniform(0.35, 0.65, N).astype(np.float32)
    return d

def reference(tab_words, tab_scales, offs, tab2_words, tab2_scales, offs2, pos1, w1, base, w2_words, w2_scales, wgs, w4_words, w4_scales, am):
    v = unpack_weight(tab_words, tab_scales, "e4m3")[:, unstriped(offs)]
    v2 = unpack_weight(tab2_words, tab2_scales, "e4m3")[:, unstriped(offs2)]
    a = (mxq(f64(w1), 0, "e4m3").T @ v) + f64(base)
    x = unpack_weight(w2_words, w2_scales, "e4m3").T @ v2
    b = 1.0 / (1.0 + np.exp(-x))
    placed = np.zeros((H, S))
    placed[:, unstriped(pos1)] = np.tile(f64(wgs), (H // 128, 1)) * b
    z = a * (1.0 + placed)
    y = unpack_weight(w4_words, w4_scales, "e2m1").T @ mxq(z, 0, "e4m3")
    return y - f64(am)[:, None] * np.sin(y)

@@ -1,0 +1,309 @@
+from contextlib import ExitStack
+
+import concourse.mybir as mybir
+from concourse.masks import make_identity
+
+FLOPS = 3758096384
+
+K, K2, H, N, T, S, T2, L = 1024, 512, 1024, 512, 4096, 1024, 2048, 512
+
+F32 = mybir.dt.float32
+BF16 = mybir.dt.bfloat16
+I32 = mybir.dt.int32
+U32 = mybir.dt.uint32
+U16 = mybir.dt.uint16
+U8 = mybir.dt.uint8
+FP8X4 = mybir.dt.float8_e4m3fn_x4
+FP4X4 = mybir.dt.float4_e2m1fn_x4
+MULT = mybir.AluOpType.mult
+ADD = mybir.AluOpType.add
+SIGMOID = mybir.ActivationFunctionType.Sigmoid
+SIN = mybir.ActivationFunctionType.Sin
+
+P = 128
+HALF = 512
+CHUNK = 256
+
+
+def tile_list_vending_refill_urgency_kernel(
+    tc, tab_words, tab_scales, offs, tab2_words, tab2_scales, offs2, pos1, w1, base,
+    w2_words, w2_scales, wgs, w4_words, w4_scales, am, out,
+):
+    nc = tc.nc
+    with ExitStack() as ctx:
+        keep = ctx.enter_context(tc.tile_pool(name="keep", bufs=1))
+        ring = ctx.enter_context(tc.tile_pool(name="ring", bufs=1))
+        psum = ctx.enter_context(tc.psum_pool(name="psum", bufs=4))
+
+        idx = keep.tile([P, S // 16], U16, name="idx")
+        idx2 = keep.tile([P, L // 16], U16, name="idx2")
+        pos = keep.tile([P, L // 16], U16, name="pos")
+
+        def held(shape, dtype, name):
+            return keep.tile(shape, dtype, name=name, align_bytes=64)
+
+        t2s = held([P, T2], U8, "t2s")
+        w2s_raw = held([P, H], U8, "w2s_raw")
+        ts = held([P, T], U8, "ts")
+        w4s = held([P, 2, N], U8, "w4s")
+        pages = [held([P, S], F32, f"page{t}") for t in range(4)]
+        nc.vector.memset(t2s[:].bitcast(I32), 0)
+        nc.vector.memset(w2s_raw[:].bitcast(I32), 0)
+        nc.vector.memset(ts[:].bitcast(I32), 0)
+        nc.vector.memset(w4s[:].rearrange("p a n -> p (a n)").bitcast(I32), 0)
+        nc.vector.memset(pages[0][:], 0.0)
+
+        t2w = held([P, T2], I32, "t2w")
+        w2w_raw = held([P, H], I32, "w2w_raw")
+        nc.sync.dma_start(idx2[:], offs2)
+        nc.sync.dma_start(pos[:], pos1)
+        for q in range(4):
+            nc.sync.dma_start(t2s[32 * q : 32 * q + 4, :].bitcast(I32), tab2_scales[0, 4 * q : 4 * q + 4, :].bitcast(I32))
+        nc.sync.dma_start(t2w[:], tab2_words[0].rearrange("p t i -> p (t i)").bitcast(I32))
+        nc.sync.dma_start(w2w_raw[:], w2_words[0].rearrange("p t i -> p (t i)").bitcast(I32))
+        for q in range(4):
+            nc.sync.dma_start(w2s_raw[32 * q : 32 * q + 4, :].bitcast(I32), w2_scales[0, 4 * q : 4 * q + 4, :].bitcast(I32))
+        wg = held([P, 4, L], F32, "wg")
+        for q in range(4):
+            nc.sync.dma_start(wg[32 * q : 32 * q + 32, :, :], wgs.rearrange("(m t) j -> m t j", t=4))
+
+        def load_w1(b, a):
+            raw = ring.tile([P, 4, 512], F32, name="w1raw", bufs=2)
+            nc.sync.dma_start(raw[:], w1[512 * a : 512 * a + 512, 512 * b : 512 * b + 512].rearrange("(p i) c -> p i c", i=4))
+            return raw
+
+        def load_base(b):
+            rows = held([P, 4, S], F32, f"base{b}")
+            nc.sync.dma_start(rows[:], base[512 * b : 512 * b + 512, :].rearrange("(p t) j -> p t j", t=4))
+            return rows
+
+        w1raw = {(0, a): load_w1(0, a) for a in range(2)}
+        base_rows = [load_base(0)]
+        tw = [held([P, T], I32, f"tw{a}") for a in range(2)]
+        for a in range(2):
+            nc.sync.dma_start(tw[a][:], tab_words[a].rearrange("p t i -> p (t i)").bitcast(I32))
+        for q in range(4):
+            nc.sync.dma_start(ts[32 * q : 32 * q + 8, :].bitcast(I32), tab_scales[:, 4 * q : 4 * q + 4, :].bitcast(I32))
+        nc.sync.dma_start(idx[:], offs)
+        ident = held([P, P], F32, "ident")
+        make_identity(nc, ident[:])
+
+        v2w = held([P, L], U32, "v2w")
+        v2s = held([P, L], U8, "v2s")
+        nc.vector.tensor_copy(v2w[:], t2w[:].bitcast(U32).indirect(idx2[:]))
+        nc.vector.tensor_copy(v2s[:], t2s[:].indirect(idx2[:]))
+        w2w, w2s, gates = {}, {}, {}
+
+        def deal(dst, src, b):
+            cols = slice(512 * b, 512 * b + 512)
+            nc.vector.tensor_copy(dst[:].rearrange("p (t m) -> p m t", t=4), src[:, cols].rearrange("p (m t) -> p m t", t=4))
+
+        def camera(s):
+            b, t = divmod(s, 4)
+            cols = slice(P * t, P * t + P)
+            x = psum.tile([P, 512], F32, name="acc")
+            nc.tensor.matmul_mx(
+                out=x[:], lhsT=w2w[b][:, cols].bitcast(FP8X4), lhsT_scale=w2s[b][:, cols],
+                rhs=v2w[:].bitcast(FP8X4), rhs_scale=v2s[:], start=True, stop=True,
+            )
+            gates[s] = ring.tile([P, 512], F32, name="f32row", bufs=12)
+            nc.scalar.activation(gates[s][:], x[:], SIGMOID)
+
+        def place(s):
+            nc.vector.tensor_tensor(page_of[s][:].indirect(pos[:]), gates[s][:], wg[:, s % 4, :], MULT)
+
+        w2w[0] = held([P, 512], I32, "w2w0")
+        deal(w2w[0], w2w_raw, 0)
+        for b in range(2):
+            w2s[b] = held([P, 512], U8, f"w2s{b}")
+            deal(w2s[b], w2s_raw, b)
+        pages.append(held([P, S], F32, "t2s"))
+        pages.append(held([P, S], F32, "w2s_raw"))
+        page_of = [pages[s % 6] for s in range(8)]
+        for page in pages[1:]:
+            nc.vector.memset(page[:], 0.0)
+        for s in range(4):
+            camera(s)
+
+        def weave_w1(raw):
+            woven = ring.tile([P, 2048], BF16, name="woven", bufs=3, align_bytes=64)
+            nc.scalar.copy(
+                woven[:].rearrange("p (t m i) -> p m i t", t=4, i=4),
+                raw[:].rearrange("p i (m t) -> p m i t", t=4),
+            )
+            return woven
+
+        def quantise(src, width, name):
+            codes = held([P, width], U32, name + "c")
+            scales = held([P, width], U8, name + "s")
+            nc.vector.quantize_mx(out=codes[:].bitcast(FP8X4), scales=scales[:], in_=src)
+            return codes, scales
+
+        w1woven = {(0, a): weave_w1(w1raw[0, a]) for a in range(2)}
+        base_rows.append(load_base(1))
+        for a in range(2):
+            w1raw[1, a] = load_w1(1, a)
+        w4w = held([P, 2, 2 * N], U8, "w4w")
+        nc.sync.dma_start(w4w[:].bitcast(I32), w4_words.rearrange("a p c -> p a c").bitcast(I32))
+        for q in range(4):
+            nc.sync.dma_start(
+                w4s[32 * q : 32 * q + 4, :, :].bitcast(I32),
+                w4_scales[:, 4 * q : 4 * q + 4, :].rearrange("a r c -> r a c").bitcast(I32),
+            )
+        amp = held([P, 4], F32, "amp")
+        with nc.allow_non_contiguous_dma(reason="one value of am to a partition"):
+            nc.sync.dma_start(amp[:], am.rearrange("(i p) -> p i", p=P))
+
+        base_t = []
+        for g in range(8):
+            bank = psum.tile([P, 4, P], F32, name="y")
+            for t in range(4):
+                nc.tensor.transpose(bank[:, t, :], base_rows[0][:, t, P * g : P * g + P], ident[:])
+            turned = ring.tile([P, 4, P], F32, name="f32row", bufs=12)
+            nc.scalar.copy(turned[:], bank[:])
+            base_t.append(turned)
+
+        for s in range(4):
+            place(s)
+        w1q = {(0, a): quantise(w1woven[0, a][:], 512, f"w1q0{a}") for a in range(2)}
+
+        vw, vs = {}, {}
+
+        def pick_scales(h):
+            vs[h] = held([P, HALF], U8, f"vs{h}")
+            nc.vector.tensor_copy(vs[h][:], ts[:].indirect(idx[:, 32 * h : 32 * h + 32]))
+
+        def pick_words(h):
+            for a in range(2):
+                vw[a, h] = held([P, HALF], U32, f"vw{a}{h}")
+                nc.vector.tensor_copy(vw[a, h][:], tw[a][:].bitcast(U32).indirect(idx[:, 32 * h : 32 * h + 32]))
+
+        sales_t = {}
+
+        def sales_turned(h):
+            sales_t[h] = held([P, 4, 512], F32, ("t2w", "tw0")[h])
+            for gg in range(4):
+                cols = slice(P * gg, P * gg + P)
+                bank = psum.tile([P, 512], F32, name="acc")
+                for a in range(2):
+                    codes, scales = w1q[0, a]
+                    nc.tensor.matmul_mx(
+                        out=bank[:], lhsT=vw[a, h][:, cols].bitcast(FP8X4), lhsT_scale=vs[h][4 * a : P, cols],
+                        rhs=codes[:].bitcast(FP8X4), rhs_scale=scales[:], start=(a == 0), stop=(a == 1),
+                    )
+                nc.scalar.copy(sales_t[h][:, gg, :], bank[:])
+
+        pick_scales(0)
+        pick_words(0)
+        sales_turned(0)
+        pick_scales(1)
+        w2w[1] = held([P, 512], I32, "ts")
+        deal(w2w[1], w2w_raw, 1)
+        pick_words(1)
+        for s in range(4, 8):
+            camera(s)
+        sales_turned(1)
+        place(4)
+        place(5)
+
+        def sales(dst, b, t, h, cols):
+            rows = slice(P * t, P * t + P)
+            for a in range(2):
+                codes, scales = w1q[b, a]
+                nc.tensor.matmul_mx(
+                    out=dst, lhsT=codes[:, rows].bitcast(FP8X4), lhsT_scale=scales[:, rows],
+                    rhs=vw[a, h][:, cols].bitcast(FP8X4), rhs_scale=vs[h][4 * a : P, cols],
+                    start=(a == 0), stop=(a == 1),
+                )
+
+        def weave_z(planes, cols, width):
+            woven = ring.tile([P, 4 * width], BF16, name="woven", bufs=3, align_bytes=64)
+            nc.scalar.copy(
+                woven[:].rearrange("p (c i t) -> p c t i", i=4, t=4),
+                planes[:, :, cols].rearrange("p t (c i) -> p c t i", i=4),
+            )
+            return woven
+
+        zp0 = held([P, 4, S], BF16, "zp0")
+
+        def make_z0(t):
+            for h in range(2):
+                bank = psum.tile([P, 4, P], F32, name=("acc", "y")[h])
+                for gg in range(4):
+                    nc.tensor.matmul(bank[:, gg, :], lhsT=base_t[4 * h + gg][:, t, :], rhs=ident[:], is_transpose=True, start=(gg == 0), stop=False)
+                for gg in range(4):
+                    nc.tensor.matmul(bank[:, gg, :], lhsT=sales_t[h][:, gg, P * t : P * t + P], rhs=ident[:], is_transpose=True, start=False, stop=(gg == 3))
+                cols = slice(HALF * h, HALF * h + HALF)
+                nc.vector.scalar_tensor_tensor(zp0[:, t, cols], page_of[t][:, cols], 1.0, bank[:].rearrange("p g j -> p (g j)"), ADD, MULT)
+
+        make_z0(0)
+        make_z0(1)
+        place(6)
+        make_z0(2)
+        make_z0(3)
+        for a in range(2):
+            w1q[1, a] = quantise(weave_w1(w1raw[1, a])[:], 512, f"w1q1{a}")
+        place(7)
+        zq0 = []
+        for h in range(2):
+            woven = weave_z(zp0, slice(HALF * h, HALF * h + HALF), HALF)
+            zq0.append(quantise(woven[:], HALF, f"zq0{h}"))
+
+        out_view = out.rearrange("(i p) j -> p i j", p=P)
+
+        def make_z(c):
+            h, cc = divmod(c, 2)
+            local = slice(CHUNK * cc, CHUNK * cc + CHUNK)
+            cols = slice(CHUNK * c, CHUNK * c + CHUNK)
+            summed = ring.tile([P, 4, CHUNK], F32, name="summed", bufs=2)
+            for u in range(2):
+                acc = psum.tile([P, 2, CHUNK], F32, name="acc")
+                for e in range(2):
+                    sales(acc[:, e, :], 1, 2 * u + e, h, local)
+                nc.vector.tensor_tensor(summed[:, 2 * u : 2 * u + 2, :], acc[:], base_rows[1][:, 2 * u : 2 * u + 2, cols], ADD)
+            planes = ring.tile([P, 4, CHUNK], BF16, name="zp1", bufs=2)
+            for t in range(4):
+                nc.vector.scalar_tensor_tensor(planes[:, t, :], page_of[4 + t][:, cols], 1.0, summed[:, t, :], ADD, MULT)
+            return weave_z(planes, slice(0, CHUNK), CHUNK)
+
+        def score(c, woven):
+            h, cc = divmod(c, 2)
+            zq1 = quantise(woven[:], CHUNK, f"zq1{c}")
+            banks = []
+            for u in range(2):
+                y = psum.tile([P, 2, CHUNK], F32, name="y")
+                steps = [(a, e, g) for a in range(2) for e in range(2) for g in range(2)]
+                for n_step, (a, e, g) in enumerate(steps):
+                    i = 2 * u + e
+                    codes, scales = zq0[h] if a == 0 else zq1
+                    first = (CHUNK * cc if a == 0 else 0) + P * g
+                    nc.tensor.matmul_mx(
+                        out=y[:, e, P * g : P * g + P],
+                        lhsT=w4w[:, a, 2 * P * i : 2 * P * i + 2 * P].bitcast(FP4X4),
+                        lhsT_scale=w4s[:, a, P * i : P * i + P],
+                        rhs=codes[:, first : first + P].bitcast(FP8X4), rhs_scale=scales[:, first : first + P],
+                        start=(n_step == 0), stop=(n_step == len(steps) - 1),
+                    )
+                neg_sin = ring.tile([P, 2, CHUNK], F32, name="f32row", bufs=12)
+                nc.scalar.activation(neg_sin[:], y[:], SIN, scale=-1.0)
+                banks.append((y, neg_sin))
+            return banks
+
+        def finish(c, banks):
+            cols = slice(CHUNK * c, CHUNK * c + CHUNK)
+            for u, (y, neg_sin) in enumerate(banks):
+                res = ring.tile([P, 2, CHUNK], F32, name="f32row", bufs=12)
+                for e in range(2):
+                    i = 2 * u + e
+                    nc.vector.scalar_tensor_tensor(res[:, e, :], neg_sin[:, e, :], amp[:, i : i + 1], y[:, e, :], MULT, ADD)
+                nc.sync.dma_start(out_view[:, 2 * u : 2 * u + 2, cols], res[:])
+
+        chunks = S // CHUNK
+        woven_z, scored = {}, {}
+        for step in range(chunks + 2):
+            if step < chunks:
+                woven_z[step] = make_z(step)
+            if 0 <= step - 1 < chunks:
+                scored[step - 1] = score(step - 1, woven_z[step - 1])
+            if 0 <= step - 2 < chunks:
+                finish(step - 2, scored[step - 2])

@@ -46,26 +46,24 @@ def tile_list_vending_refill_urgency_kernel(
         w2s_raw = held([P, H], U8, "w2s_raw")
         ts = held([P, T], U8, "ts")
         w4s = held([P, 2, N], U8, "w4s")
-        pages = [held([P, S], F32, f"page{t}") for t in range(4)]
-        nc.vector.memset(t2s[:].bitcast(I32), 0)
+        pages = [held([P, S], F32, f"page{t}") for t in range(2)]
         nc.vector.memset(w2s_raw[:].bitcast(I32), 0)
+        nc.vector.memset(t2s[:].bitcast(I32), 0)
+        nc.vector.memset(pages[0][:].bitcast(I32), 0)
         nc.vector.memset(ts[:].bitcast(I32), 0)
-        nc.vector.memset(w4s[:].rearrange("p a n -> p (a n)").bitcast(I32), 0)
-        nc.vector.memset(pages[0][:], 0.0)
 
         t2w = held([P, T2], I32, "t2w")
         w2w_raw = held([P, H], I32, "w2w_raw")
         nc.sync.dma_start(idx2[:], offs2)
+        wg_raw = held([P, L], F32, "wg_raw")
+        nc.sync.dma_start(wg_raw[:], wgs)
         nc.sync.dma_start(pos[:], pos1)
         for q in range(4):
-            nc.sync.dma_start(t2s[32 * q : 32 * q + 4, :].bitcast(I32), tab2_scales[0, 4 * q : 4 * q + 4, :].bitcast(I32))
-        nc.sync.dma_start(t2w[:], tab2_words[0].rearrange("p t i -> p (t i)").bitcast(I32))
-        nc.sync.dma_start(w2w_raw[:], w2_words[0].rearrange("p t i -> p (t i)").bitcast(I32))
-        for q in range(4):
             nc.sync.dma_start(w2s_raw[32 * q : 32 * q + 4, :].bitcast(I32), w2_scales[0, 4 * q : 4 * q + 4, :].bitcast(I32))
-        wg = held([P, 4, L], F32, "wg")
+        nc.sync.dma_start(t2w[:], tab2_words[0].rearrange("p t i -> p (t i)").bitcast(I32))
         for q in range(4):
-            nc.sync.dma_start(wg[32 * q : 32 * q + 32, :, :], wgs.rearrange("(m t) j -> m t j", t=4))
+            nc.sync.dma_start(t2s[32 * q : 32 * q + 4, :].bitcast(I32), tab2_scales[0, 4 * q : 4 * q + 4, :].bitcast(I32))
+        nc.sync.dma_start(w2w_raw[:], w2_words[0].rearrange("p t i -> p (t i)").bitcast(I32))
 
         def load_w1(b, a):
             raw = ring.tile([P, 4, 512], F32, name="w1raw", bufs=2)
@@ -73,20 +71,39 @@ def tile_list_vending_refill_urgency_kernel(
             return raw
 
         def load_base(b):
-            rows = held([P, 4, S], F32, f"base{b}")
+            rows = held([P, 4, S], F32, "base_rows")
             nc.sync.dma_start(rows[:], base[512 * b : 512 * b + 512, :].rearrange("(p t) j -> p t j", t=4))
             return rows
 
         w1raw = {(0, a): load_w1(0, a) for a in range(2)}
         base_rows = [load_base(0)]
+        for q in range(4):
+            nc.sync.dma_start(ts[32 * q : 32 * q + 8, :].bitcast(I32), tab_scales[:, 4 * q : 4 * q + 4, :].bitcast(I32))
         tw = [held([P, T], I32, f"tw{a}") for a in range(2)]
         for a in range(2):
             nc.sync.dma_start(tw[a][:], tab_words[a].rearrange("p t i -> p (t i)").bitcast(I32))
-        for q in range(4):
-            nc.sync.dma_start(ts[32 * q : 32 * q + 8, :].bitcast(I32), tab_scales[:, 4 * q : 4 * q + 4, :].bitcast(I32))
         nc.sync.dma_start(idx[:], offs)
         ident = held([P, P], F32, "ident")
         make_identity(nc, ident[:])
+
+        wg_turned = psum.tile([P, 4, P], F32, name="y")
+        for g in range(4):
+            nc.tensor.transpose(wg_turned[:, g, :], wg_raw[:, P * g : P * g + P], ident[:])
+        wg, dealt = {}, {}
+
+        def deal_rows(pair, slot, copy):
+            dealt[pair] = held([P, 2, 4, 4, 32], F32, slot)
+            rows = wg_turned[:].rearrange("p g (u q t) -> p g u q t", u=1, t=4)[:, :, :, :, 2 * pair : 2 * pair + 2]
+            copy(dealt[pair][:].rearrange("p t g u q -> p g u q t"), rows.broadcast_to([P, 4, 4, 32, 2]))
+
+        def turn_back(t, slot, copy):
+            back = psum.tile([P, 4, P], F32, name=slot)
+            for g in range(4):
+                nc.tensor.transpose(back[:, g, :], dealt[t // 2][:, t % 2, g, :, :].rearrange("p u q -> p (u q)"), ident[:])
+            wg[t] = held([P, L], F32, f"wg{t}")
+            copy(wg[t][:], back[:].rearrange("p g j -> p (g j)"))
+
+        deal_rows(0, "dealt", nc.vector.tensor_copy)
 
         v2w = held([P, L], U32, "v2w")
         v2s = held([P, L], U8, "v2s")
@@ -106,27 +123,40 @@ def tile_list_vending_refill_urgency_kernel(
                 out=x[:], lhsT=w2w[b][:, cols].bitcast(FP8X4), lhsT_scale=w2s[b][:, cols],
                 rhs=v2w[:].bitcast(FP8X4), rhs_scale=v2s[:], start=True, stop=True,
             )
-            gates[s] = ring.tile([P, 512], F32, name="f32row", bufs=12)
+            gates[s] = ring.tile([P, 512], F32, name="f32row", bufs=16)
             nc.scalar.activation(gates[s][:], x[:], SIGMOID)
 
         def place(s):
-            nc.vector.tensor_tensor(page_of[s][:].indirect(pos[:]), gates[s][:], wg[:, s % 4, :], MULT)
+            nc.vector.tensor_tensor(pages[s][:].indirect(pos[:]), gates[s][:], wg[s % 4][:], MULT)
 
-        w2w[0] = held([P, 512], I32, "w2w0")
-        deal(w2w[0], w2w_raw, 0)
+        def late_page(slot):
+            page = held([P, S], F32, slot)
+            nc.gpsimd.memset(page[:].bitcast(I32), 0)
+            pages.append(page)
+
         for b in range(2):
+            w2w[b] = held([P, 512], I32, f"w2w{b}")
             w2s[b] = held([P, 512], U8, f"w2s{b}")
-            deal(w2s[b], w2s_raw, b)
-        pages.append(held([P, S], F32, "t2s"))
-        pages.append(held([P, S], F32, "w2s_raw"))
-        page_of = [pages[s % 6] for s in range(8)]
-        for page in pages[1:]:
-            nc.vector.memset(page[:], 0.0)
+        deal(w2s[0], w2s_raw, 0)
+        deal(w2s[1], w2s_raw, 1)
+        deal(w2w[0], w2w_raw, 0)
+        deal(w2w[1], w2w_raw, 1)
+        turn_back(0, "y", nc.vector.tensor_copy)
+        nc.vector.memset(pages[1][:].bitcast(I32), 0)
+        nc.vector.memset(w4s[:].rearrange("p a n -> p (a n)").bitcast(I32), 0)
         for s in range(4):
             camera(s)
+        turn_back(1, "acc", nc.scalar.copy)
+        deal_rows(1, "w2w0", nc.scalar.copy)
+        for s in range(4, 8):
+            camera(s)
+        for t in range(2, 4):
+            turn_back(t, "acc", nc.scalar.copy)
+        for slot in ("w2w_raw", "w2s0", "v2s"):
+            late_page(slot)
 
-        def weave_w1(raw):
-            woven = ring.tile([P, 2048], BF16, name="woven", bufs=3, align_bytes=64)
+        def weave_w1(raw, slot):
+            woven = held([P, 2048], BF16, slot)
             nc.scalar.copy(
                 woven[:].rearrange("p (t m i) -> p m i t", t=4, i=4),
                 raw[:].rearrange("p i (m t) -> p m i t", t=4),
@@ -139,7 +169,7 @@ def tile_list_vending_refill_urgency_kernel(
             nc.vector.quantize_mx(out=codes[:].bitcast(FP8X4), scales=scales[:], in_=src)
             return codes, scales
 
-        w1woven = {(0, a): weave_w1(w1raw[0, a]) for a in range(2)}
+        w1woven = {(0, a): weave_w1(w1raw[0, a], ("v2w", "w2w1")[a]) for a in range(2)}
         base_rows.append(load_base(1))
         for a in range(2):
             w1raw[1, a] = load_w1(1, a)
@@ -156,14 +186,14 @@ def tile_list_vending_refill_urgency_kernel(
 
         base_t = []
         for g in range(8):
-            bank = psum.tile([P, 4, P], F32, name="y")
+            bank = psum.tile([P, 4, P], F32, name="acc")
             for t in range(4):
                 nc.tensor.transpose(bank[:, t, :], base_rows[0][:, t, P * g : P * g + P], ident[:])
-            turned = ring.tile([P, 4, P], F32, name="f32row", bufs=12)
+            turned = ring.tile([P, 4, P], F32, name="f32row", bufs=16)
             nc.scalar.copy(turned[:], bank[:])
             base_t.append(turned)
 
-        for s in range(4):
+        for s in range(5):
             place(s)
         w1q = {(0, a): quantise(w1woven[0, a][:], 512, f"w1q0{a}") for a in range(2)}
 
@@ -197,14 +227,12 @@ def tile_list_vending_refill_urgency_kernel(
         pick_words(0)
         sales_turned(0)
         pick_scales(1)
-        w2w[1] = held([P, 512], I32, "ts")
-        deal(w2w[1], w2w_raw, 1)
+        late_page("ts")
         pick_words(1)
-        for s in range(4, 8):
-            camera(s)
+        late_page("tw1")
         sales_turned(1)
-        place(4)
         place(5)
+        place(6)
 
         def sales(dst, b, t, h, cols):
             rows = slice(P * t, P * t + P)
@@ -217,37 +245,33 @@ def tile_list_vending_refill_urgency_kernel(
                 )
 
         def weave_z(planes, cols, width):
-            woven = ring.tile([P, 4 * width], BF16, name="woven", bufs=3, align_bytes=64)
+            woven = ring.tile([P, 4 * width], BF16, name="woven", bufs=4, align_bytes=64)
             nc.scalar.copy(
                 woven[:].rearrange("p (c i t) -> p c t i", i=4, t=4),
                 planes[:, :, cols].rearrange("p t (c i) -> p c t i", i=4),
             )
             return woven
 
-        zp0 = held([P, 4, S], BF16, "zp0")
 
-        def make_z0(t):
-            for h in range(2):
-                bank = psum.tile([P, 4, P], F32, name=("acc", "y")[h])
+        def make_z0(h):
+            planes = ring.tile([P, 4, HALF], BF16, name="zp0", bufs=2)
+            for t in range(4):
+                bank = psum.tile([P, 4, P], F32, name=("y", "acc")[h])
                 for gg in range(4):
                     nc.tensor.matmul(bank[:, gg, :], lhsT=base_t[4 * h + gg][:, t, :], rhs=ident[:], is_transpose=True, start=(gg == 0), stop=False)
                 for gg in range(4):
                     nc.tensor.matmul(bank[:, gg, :], lhsT=sales_t[h][:, gg, P * t : P * t + P], rhs=ident[:], is_transpose=True, start=False, stop=(gg == 3))
                 cols = slice(HALF * h, HALF * h + HALF)
-                nc.vector.scalar_tensor_tensor(zp0[:, t, cols], page_of[t][:, cols], 1.0, bank[:].rearrange("p g j -> p (g j)"), ADD, MULT)
+                nc.vector.scalar_tensor_tensor(planes[:, t, :], pages[t][:, cols], 1.0, bank[:].rearrange("p g j -> p (g j)"), ADD, MULT)
+            return weave_z(planes, slice(0, HALF), HALF)
 
-        make_z0(0)
-        make_z0(1)
-        place(6)
-        make_z0(2)
-        make_z0(3)
-        for a in range(2):
-            w1q[1, a] = quantise(weave_w1(w1raw[1, a])[:], 512, f"w1q1{a}")
+        z0_woven = [make_z0(0)]
+        late_page("t2w")
         place(7)
-        zq0 = []
-        for h in range(2):
-            woven = weave_z(zp0, slice(HALF * h, HALF * h + HALF), HALF)
-            zq0.append(quantise(woven[:], HALF, f"zq0{h}"))
+        for a in range(2):
+            w1q[1, a] = quantise(weave_w1(w1raw[1, a], ("v2w", "w2w1")[a])[:], 512, f"w1q1{a}")
+        z0_woven.append(make_z0(1))
+        zq0 = {}
 
         out_view = out.rearrange("(i p) j -> p i j", p=P)
 
@@ -263,11 +287,13 @@ def tile_list_vending_refill_urgency_kernel(
                 nc.vector.tensor_tensor(summed[:, 2 * u : 2 * u + 2, :], acc[:], base_rows[1][:, 2 * u : 2 * u + 2, cols], ADD)
             planes = ring.tile([P, 4, CHUNK], BF16, name="zp1", bufs=2)
             for t in range(4):
-                nc.vector.scalar_tensor_tensor(planes[:, t, :], page_of[4 + t][:, cols], 1.0, summed[:, t, :], ADD, MULT)
+                nc.vector.scalar_tensor_tensor(planes[:, t, :], pages[4 + t][:, cols], 1.0, summed[:, t, :], ADD, MULT)
             return weave_z(planes, slice(0, CHUNK), CHUNK)
 
         def score(c, woven):
             h, cc = divmod(c, 2)
+            if cc == 0:
+                zq0[h] = quantise(z0_woven[h][:], HALF, f"zq0{h}")
             zq1 = quantise(woven[:], CHUNK, f"zq1{c}")
             banks = []
             for u in range(2):
@@ -284,7 +310,7 @@ def tile_list_vending_refill_urgency_kernel(
                         rhs=codes[:, first : first + P].bitcast(FP8X4), rhs_scale=scales[:, first : first + P],
                         start=(n_step == 0), stop=(n_step == len(steps) - 1),
                     )
-                neg_sin = ring.tile([P, 2, CHUNK], F32, name="f32row", bufs=12)
+                neg_sin = ring.tile([P, 2, CHUNK], F32, name="f32row", bufs=16)
                 nc.scalar.activation(neg_sin[:], y[:], SIN, scale=-1.0)
                 banks.append((y, neg_sin))
             return banks
@@ -292,7 +318,7 @@ def tile_list_vending_refill_urgency_kernel(
         def finish(c, banks):
             cols = slice(CHUNK * c, CHUNK * c + CHUNK)
             for u, (y, neg_sin) in enumerate(banks):
-                res = ring.tile([P, 2, CHUNK], F32, name="f32row", bufs=12)
+                res = ring.tile([P, 2, CHUNK], F32, name="f32row", bufs=16)
                 for e in range(2):
                     i = 2 * u + e
                     nc.vector.scalar_tensor_tensor(res[:, e, :], neg_sin[:, e, :], amp[:, i : i + 1], y[:, e, :], MULT, ADD)

@@ -44,26 +44,25 @@ def tile_list_vending_refill_urgency_kernel(
 
         t2s = held([P, T2], U8, "t2s")
         w2s_raw = held([P, H], U8, "w2s_raw")
-        ts = held([P, T], U8, "ts")
-        w4s = held([P, 2, N], U8, "w4s")
-        pages = [held([P, S], F32, f"page{t}") for t in range(2)]
-        nc.vector.memset(w2s_raw[:].bitcast(I32), 0)
+        pages = [held([P, S], F32, "page0")]
         nc.vector.memset(t2s[:].bitcast(I32), 0)
         nc.vector.memset(pages[0][:].bitcast(I32), 0)
-        nc.vector.memset(ts[:].bitcast(I32), 0)
 
         t2w = held([P, T2], I32, "t2w")
         w2w_raw = held([P, H], I32, "w2w_raw")
         nc.sync.dma_start(idx2[:], offs2)
         wg_raw = held([P, L], F32, "wg_raw")
         nc.sync.dma_start(wg_raw[:], wgs)
-        nc.sync.dma_start(pos[:], pos1)
-        for q in range(4):
-            nc.sync.dma_start(w2s_raw[32 * q : 32 * q + 4, :].bitcast(I32), w2_scales[0, 4 * q : 4 * q + 4, :].bitcast(I32))
         nc.sync.dma_start(t2w[:], tab2_words[0].rearrange("p t i -> p (t i)").bitcast(I32))
+        nc.sync.dma_start(w2w_raw[:], w2_words[0].rearrange("p t i -> p (t i)").bitcast(I32))
         for q in range(4):
             nc.sync.dma_start(t2s[32 * q : 32 * q + 4, :].bitcast(I32), tab2_scales[0, 4 * q : 4 * q + 4, :].bitcast(I32))
-        nc.sync.dma_start(w2w_raw[:], w2_words[0].rearrange("p t i -> p (t i)").bitcast(I32))
+        nc.sync.dma_start(pos[:], pos1)
+        ident = held([P, P], F32, "ident")
+        make_identity(nc, ident[:])
+        nc.gpsimd.memset(w2s_raw[:].bitcast(I32), 0)
+        for q in range(4):
+            nc.gpsimd.dma_start(w2s_raw[32 * q : 32 * q + 4, :].bitcast(I32), w2_scales[0, 4 * q : 4 * q + 4, :].bitcast(I32))
 
         def load_w1(b, a):
             raw = ring.tile([P, 4, 512], F32, name="w1raw", bufs=2)
@@ -77,14 +76,10 @@ def tile_list_vending_refill_urgency_kernel(
 
         w1raw = {(0, a): load_w1(0, a) for a in range(2)}
         base_rows = [load_base(0)]
-        for q in range(4):
-            nc.sync.dma_start(ts[32 * q : 32 * q + 8, :].bitcast(I32), tab_scales[:, 4 * q : 4 * q + 4, :].bitcast(I32))
         tw = [held([P, T], I32, f"tw{a}") for a in range(2)]
         for a in range(2):
             nc.sync.dma_start(tw[a][:], tab_words[a].rearrange("p t i -> p (t i)").bitcast(I32))
         nc.sync.dma_start(idx[:], offs)
-        ident = held([P, P], F32, "ident")
-        make_identity(nc, ident[:])
 
         wg_turned = psum.tile([P, 4, P], F32, name="y")
         for g in range(4):
@@ -137,13 +132,11 @@ def tile_list_vending_refill_urgency_kernel(
         for b in range(2):
             w2w[b] = held([P, 512], I32, f"w2w{b}")
             w2s[b] = held([P, 512], U8, f"w2s{b}")
+        deal(w2w[0], w2w_raw, 0)
         deal(w2s[0], w2s_raw, 0)
         deal(w2s[1], w2s_raw, 1)
-        deal(w2w[0], w2w_raw, 0)
         deal(w2w[1], w2w_raw, 1)
         turn_back(0, "y", nc.vector.tensor_copy)
-        nc.vector.memset(pages[1][:].bitcast(I32), 0)
-        nc.vector.memset(w4s[:].rearrange("p a n -> p (a n)").bitcast(I32), 0)
         for s in range(4):
             camera(s)
         turn_back(1, "acc", nc.scalar.copy)
@@ -152,8 +145,19 @@ def tile_list_vending_refill_urgency_kernel(
             camera(s)
         for t in range(2, 4):
             turn_back(t, "acc", nc.scalar.copy)
-        for slot in ("w2w_raw", "w2s0", "v2s"):
+        for slot in ("wg_raw", "w2w_raw", "w2s0", "dealt"):
             late_page(slot)
+        ts = held([P, T], U8, "v2s")
+        nc.gpsimd.memset(ts[:].bitcast(I32), 0)
+        for q in range(4):
+            nc.gpsimd.dma_start(ts[32 * q : 32 * q + 8, :].bitcast(I32), tab_scales[:, 4 * q : 4 * q + 4, :].bitcast(I32))
+        w4s = held([P, 2, N], U8, "w2s1")
+        nc.gpsimd.memset(w4s[:].rearrange("p a n -> p (a n)").bitcast(I32), 0)
+        for q in range(4):
+            nc.gpsimd.dma_start(
+                w4s[32 * q : 32 * q + 4, :, :].bitcast(I32),
+                w4_scales[:, 4 * q : 4 * q + 4, :].rearrange("a r c -> r a c").bitcast(I32),
+            )
 
         def weave_w1(raw, slot):
             woven = held([P, 2048], BF16, slot)
@@ -170,16 +174,11 @@ def tile_list_vending_refill_urgency_kernel(
             return codes, scales
 
         w1woven = {(0, a): weave_w1(w1raw[0, a], ("v2w", "w2w1")[a]) for a in range(2)}
-        base_rows.append(load_base(1))
         for a in range(2):
             w1raw[1, a] = load_w1(1, a)
+        base_rows.append(load_base(1))
         w4w = held([P, 2, 2 * N], U8, "w4w")
         nc.sync.dma_start(w4w[:].bitcast(I32), w4_words.rearrange("a p c -> p a c").bitcast(I32))
-        for q in range(4):
-            nc.sync.dma_start(
-                w4s[32 * q : 32 * q + 4, :, :].bitcast(I32),
-                w4_scales[:, 4 * q : 4 * q + 4, :].rearrange("a r c -> r a c").bitcast(I32),
-            )
         amp = held([P, 4], F32, "amp")
         with nc.allow_non_contiguous_dma(reason="one value of am to a partition"):
             nc.sync.dma_start(amp[:], am.rearrange("(i p) -> p i", p=P))
@@ -227,7 +226,7 @@ def tile_list_vending_refill_urgency_kernel(
         pick_words(0)
         sales_turned(0)
         pick_scales(1)
-        late_page("ts")
+        late_page("v2s")
         pick_words(1)
         late_page("tw1")
         sales_turned(1)
@@ -269,7 +268,7 @@ def tile_list_vending_refill_urgency_kernel(
         late_page("t2w")
         place(7)
         for a in range(2):
-            w1q[1, a] = quantise(weave_w1(w1raw[1, a], ("v2w", "w2w1")[a])[:], 512, f"w1q1{a}")
+            w1q[1, a] = quantise(weave_w1(w1raw[1, a], ("v2w", "w1q00c")[a])[:], 512, f"w1q1{a}")
         z0_woven.append(make_z0(1))
         zq0 = {}
 
@@ -281,7 +280,7 @@ def tile_list_vending_refill_urgency_kernel(
             cols = slice(CHUNK * c, CHUNK * c + CHUNK)
             summed = ring.tile([P, 4, CHUNK], F32, name="summed", bufs=2)
             for u in range(2):
-                acc = psum.tile([P, 2, CHUNK], F32, name="acc")
+                acc = psum.tile([P, 2, CHUNK], F32, name="y" if c == 0 else "acc")
                 for e in range(2):
                     sales(acc[:, e, :], 1, 2 * u + e, h, local)
                 nc.vector.tensor_tensor(summed[:, 2 * u : 2 * u + 2, :], acc[:], base_rows[1][:, 2 * u : 2 * u + 2, cols], ADD)

from contextlib import ExitStack

import concourse.mybir as mybir
from concourse.masks import make_identity

FLOPS = 3758096384

K, K2, H, N, T, S, T2, L = 1024, 512, 1024, 512, 4096, 1024, 2048, 512

F32 = mybir.dt.float32
BF16 = mybir.dt.bfloat16
I32 = mybir.dt.int32
U32 = mybir.dt.uint32
U16 = mybir.dt.uint16
U8 = mybir.dt.uint8
FP8X4 = mybir.dt.float8_e4m3fn_x4
FP4X4 = mybir.dt.float4_e2m1fn_x4
MULT = mybir.AluOpType.mult
ADD = mybir.AluOpType.add
SIGMOID = mybir.ActivationFunctionType.Sigmoid
SIN = mybir.ActivationFunctionType.Sin

P = 128
HALF = 512
CHUNK = 256


def tile_list_vending_refill_urgency_kernel(
    tc, tab_words, tab_scales, offs, tab2_words, tab2_scales, offs2, pos1, w1, base,
    w2_words, w2_scales, wgs, w4_words, w4_scales, am, out,
):
    nc = tc.nc
    with ExitStack() as ctx:
        keep = ctx.enter_context(tc.tile_pool(name="keep", bufs=1))
        ring = ctx.enter_context(tc.tile_pool(name="ring", bufs=1))
        psum = ctx.enter_context(tc.psum_pool(name="psum", bufs=4))

        idx = keep.tile([P, S // 16], U16, name="idx")
        idx2 = keep.tile([P, L // 16], U16, name="idx2")
        pos = keep.tile([P, L // 16], U16, name="pos")

        def held(shape, dtype, name):
            return keep.tile(shape, dtype, name=name, align_bytes=64)

        t2s = held([P, T2], U8, "t2s")
        w2s_raw = held([P, H], U8, "w2s_raw")
        pages = [held([P, S], F32, "page0")]
        nc.vector.memset(t2s[:].bitcast(I32), 0)
        nc.vector.memset(pages[0][:].bitcast(I32), 0)

        t2w = held([P, T2], I32, "t2w")
        w2w_raw = held([P, H], I32, "w2w_raw")
        nc.sync.dma_start(idx2[:], offs2)
        wg_raw = held([P, L], F32, "wg_raw")
        nc.sync.dma_start(wg_raw[:], wgs)
        nc.sync.dma_start(t2w[:], tab2_words[0].rearrange("p t i -> p (t i)").bitcast(I32))
        nc.sync.dma_start(w2w_raw[:], w2_words[0].rearrange("p t i -> p (t i)").bitcast(I32))
        for q in range(4):
            nc.sync.dma_start(t2s[32 * q : 32 * q + 4, :].bitcast(I32), tab2_scales[0, 4 * q : 4 * q + 4, :].bitcast(I32))
        nc.sync.dma_start(pos[:], pos1)
        ident = held([P, P], F32, "ident")
        make_identity(nc, ident[:])
        nc.gpsimd.memset(w2s_raw[:].bitcast(I32), 0)
        for q in range(4):
            nc.gpsimd.dma_start(w2s_raw[32 * q : 32 * q + 4, :].bitcast(I32), w2_scales[0, 4 * q : 4 * q + 4, :].bitcast(I32))

        def load_w1(b, a):
            raw = ring.tile([P, 4, 512], F32, name="w1raw", bufs=2)
            nc.sync.dma_start(raw[:], w1[512 * a : 512 * a + 512, 512 * b : 512 * b + 512].rearrange("(p i) c -> p i c", i=4))
            return raw

        def load_base(b):
            rows = held([P, 4, S], F32, "base_rows")
            nc.sync.dma_start(rows[:], base[512 * b : 512 * b + 512, :].rearrange("(p t) j -> p t j", t=4))
            return rows

        w1raw = {(0, a): load_w1(0, a) for a in range(2)}
        base_rows = [load_base(0)]
        tw = [held([P, T], I32, f"tw{a}") for a in range(2)]
        for a in range(2):
            nc.sync.dma_start(tw[a][:], tab_words[a].rearrange("p t i -> p (t i)").bitcast(I32))
        nc.sync.dma_start(idx[:], offs)

        wg_turned = psum.tile([P, 4, P], F32, name="y")
        for g in range(4):
            nc.tensor.transpose(wg_turned[:, g, :], wg_raw[:, P * g : P * g + P], ident[:])
        wg, dealt = {}, {}

        def deal_rows(pair, slot, copy):
            dealt[pair] = held([P, 2, 4, 4, 32], F32, slot)
            rows = wg_turned[:].rearrange("p g (u q t) -> p g u q t", u=1, t=4)[:, :, :, :, 2 * pair : 2 * pair + 2]
            copy(dealt[pair][:].rearrange("p t g u q -> p g u q t"), rows.broadcast_to([P, 4, 4, 32, 2]))

        def turn_back(t, slot, copy):
            back = psum.tile([P, 4, P], F32, name=slot)
            for g in range(4):
                nc.tensor.transpose(back[:, g, :], dealt[t // 2][:, t % 2, g, :, :].rearrange("p u q -> p (u q)"), ident[:])
            wg[t] = held([P, L], F32, f"wg{t}")
            copy(wg[t][:], back[:].rearrange("p g j -> p (g j)"))

        deal_rows(0, "dealt", nc.vector.tensor_copy)

        v2w = held([P, L], U32, "v2w")
        v2s = held([P, L], U8, "v2s")
        nc.vector.tensor_copy(v2w[:], t2w[:].bitcast(U32).indirect(idx2[:]))
        nc.vector.tensor_copy(v2s[:], t2s[:].indirect(idx2[:]))
        w2w, w2s, gates = {}, {}, {}

        def deal(dst, src, b):
            cols = slice(512 * b, 512 * b + 512)
            nc.vector.tensor_copy(dst[:].rearrange("p (t m) -> p m t", t=4), src[:, cols].rearrange("p (m t) -> p m t", t=4))

        def camera(s):
            b, t = divmod(s, 4)
            cols = slice(P * t, P * t + P)
            x = psum.tile([P, 512], F32, name="acc")
            nc.tensor.matmul_mx(
                out=x[:], lhsT=w2w[b][:, cols].bitcast(FP8X4), lhsT_scale=w2s[b][:, cols],
                rhs=v2w[:].bitcast(FP8X4), rhs_scale=v2s[:], start=True, stop=True,
            )
            gates[s] = ring.tile([P, 512], F32, name="f32row", bufs=16)
            nc.scalar.activation(gates[s][:], x[:], SIGMOID)

        def place(s):
            nc.vector.tensor_tensor(pages[s][:].indirect(pos[:]), gates[s][:], wg[s % 4][:], MULT)

        def late_page(slot):
            page = held([P, S], F32, slot)
            nc.gpsimd.memset(page[:].bitcast(I32), 0)
            pages.append(page)

        for b in range(2):
            w2w[b] = held([P, 512], I32, f"w2w{b}")
            w2s[b] = held([P, 512], U8, f"w2s{b}")
        deal(w2w[0], w2w_raw, 0)
        deal(w2s[0], w2s_raw, 0)
        deal(w2s[1], w2s_raw, 1)
        deal(w2w[1], w2w_raw, 1)
        turn_back(0, "y", nc.vector.tensor_copy)
        for s in range(4):
            camera(s)
        turn_back(1, "acc", nc.scalar.copy)
        deal_rows(1, "w2w0", nc.scalar.copy)
        for s in range(4, 8):
            camera(s)
        for t in range(2, 4):
            turn_back(t, "acc", nc.scalar.copy)
        for slot in ("wg_raw", "w2w_raw", "w2s0", "dealt"):
            late_page(slot)
        ts = held([P, T], U8, "v2s")
        nc.gpsimd.memset(ts[:].bitcast(I32), 0)
        for q in range(4):
            nc.gpsimd.dma_start(ts[32 * q : 32 * q + 8, :].bitcast(I32), tab_scales[:, 4 * q : 4 * q + 4, :].bitcast(I32))
        w4s = held([P, 2, N], U8, "w2s1")
        nc.gpsimd.memset(w4s[:].rearrange("p a n -> p (a n)").bitcast(I32), 0)
        for q in range(4):
            nc.gpsimd.dma_start(
                w4s[32 * q : 32 * q + 4, :, :].bitcast(I32),
                w4_scales[:, 4 * q : 4 * q + 4, :].rearrange("a r c -> r a c").bitcast(I32),
            )

        def weave_w1(raw, slot):
            woven = held([P, 2048], BF16, slot)
            nc.scalar.copy(
                woven[:].rearrange("p (t m i) -> p m i t", t=4, i=4),
                raw[:].rearrange("p i (m t) -> p m i t", t=4),
            )
            return woven

        def quantise(src, width, name):
            codes = held([P, width], U32, name + "c")
            scales = held([P, width], U8, name + "s")
            nc.vector.quantize_mx(out=codes[:].bitcast(FP8X4), scales=scales[:], in_=src)
            return codes, scales

        w1woven = {(0, a): weave_w1(w1raw[0, a], ("v2w", "w2w1")[a]) for a in range(2)}
        for a in range(2):
            w1raw[1, a] = load_w1(1, a)
        base_rows.append(load_base(1))
        w4w = held([P, 2, 2 * N], U8, "w4w")
        nc.sync.dma_start(w4w[:].bitcast(I32), w4_words.rearrange("a p c -> p a c").bitcast(I32))
        amp = held([P, 4], F32, "amp")
        with nc.allow_non_contiguous_dma(reason="one value of am to a partition"):
            nc.sync.dma_start(amp[:], am.rearrange("(i p) -> p i", p=P))

        base_t = []
        for g in range(8):
            bank = psum.tile([P, 4, P], F32, name="acc")
            for t in range(4):
                nc.tensor.transpose(bank[:, t, :], base_rows[0][:, t, P * g : P * g + P], ident[:])
            turned = ring.tile([P, 4, P], F32, name="f32row", bufs=16)
            nc.scalar.copy(turned[:], bank[:])
            base_t.append(turned)

        for s in range(5):
            place(s)
        w1q = {(0, a): quantise(w1woven[0, a][:], 512, f"w1q0{a}") for a in range(2)}

        vw, vs = {}, {}

        def pick_scales(h):
            vs[h] = held([P, HALF], U8, f"vs{h}")
            nc.vector.tensor_copy(vs[h][:], ts[:].indirect(idx[:, 32 * h : 32 * h + 32]))

        def pick_words(h):
            for a in range(2):
                vw[a, h] = held([P, HALF], U32, f"vw{a}{h}")
                nc.vector.tensor_copy(vw[a, h][:], tw[a][:].bitcast(U32).indirect(idx[:, 32 * h : 32 * h + 32]))

        sales_t = {}

        def sales_turned(h):
            sales_t[h] = held([P, 4, 512], F32, ("t2w", "tw0")[h])
            for gg in range(4):
                cols = slice(P * gg, P * gg + P)
                bank = psum.tile([P, 512], F32, name="acc")
                for a in range(2):
                    codes, scales = w1q[0, a]
                    nc.tensor.matmul_mx(
                        out=bank[:], lhsT=vw[a, h][:, cols].bitcast(FP8X4), lhsT_scale=vs[h][4 * a : P, cols],
                        rhs=codes[:].bitcast(FP8X4), rhs_scale=scales[:], start=(a == 0), stop=(a == 1),
                    )
                nc.scalar.copy(sales_t[h][:, gg, :], bank[:])

        pick_scales(0)
        pick_words(0)
        sales_turned(0)
        pick_scales(1)
        late_page("v2s")
        pick_words(1)
        late_page("tw1")
        sales_turned(1)
        place(5)
        place(6)

        def sales(dst, b, t, h, cols):
            rows = slice(P * t, P * t + P)
            for a in range(2):
                codes, scales = w1q[b, a]
                nc.tensor.matmul_mx(
                    out=dst, lhsT=codes[:, rows].bitcast(FP8X4), lhsT_scale=scales[:, rows],
                    rhs=vw[a, h][:, cols].bitcast(FP8X4), rhs_scale=vs[h][4 * a : P, cols],
                    start=(a == 0), stop=(a == 1),
                )

        def weave_z(planes, cols, width):
            woven = ring.tile([P, 4 * width], BF16, name="woven", bufs=4, align_bytes=64)
            nc.scalar.copy(
                woven[:].rearrange("p (c i t) -> p c t i", i=4, t=4),
                planes[:, :, cols].rearrange("p t (c i) -> p c t i", i=4),
            )
            return woven


        def make_z0(h):
            planes = ring.tile([P, 4, HALF], BF16, name="zp0", bufs=2)
            for t in range(4):
                bank = psum.tile([P, 4, P], F32, name=("y", "acc")[h])
                for gg in range(4):
                    nc.tensor.matmul(bank[:, gg, :], lhsT=base_t[4 * h + gg][:, t, :], rhs=ident[:], is_transpose=True, start=(gg == 0), stop=False)
                for gg in range(4):
                    nc.tensor.matmul(bank[:, gg, :], lhsT=sales_t[h][:, gg, P * t : P * t + P], rhs=ident[:], is_transpose=True, start=False, stop=(gg == 3))
                cols = slice(HALF * h, HALF * h + HALF)
                nc.vector.scalar_tensor_tensor(planes[:, t, :], pages[t][:, cols], 1.0, bank[:].rearrange("p g j -> p (g j)"), ADD, MULT)
            return weave_z(planes, slice(0, HALF), HALF)

        z0_woven = [make_z0(0)]
        late_page("t2w")
        place(7)
        for a in range(2):
            w1q[1, a] = quantise(weave_w1(w1raw[1, a], ("v2w", "w1q00c")[a])[:], 512, f"w1q1{a}")
        z0_woven.append(make_z0(1))
        zq0 = {}

        out_view = out.rearrange("(i p) j -> p i j", p=P)

        def make_z(c):
            h, cc = divmod(c, 2)
            local = slice(CHUNK * cc, CHUNK * cc + CHUNK)
            cols = slice(CHUNK * c, CHUNK * c + CHUNK)
            summed = ring.tile([P, 4, CHUNK], F32, name="summed", bufs=2)
            for u in range(2):
                acc = psum.tile([P, 2, CHUNK], F32, name="y" if c == 0 else "acc")
                for e in range(2):
                    sales(acc[:, e, :], 1, 2 * u + e, h, local)
                nc.vector.tensor_tensor(summed[:, 2 * u : 2 * u + 2, :], acc[:], base_rows[1][:, 2 * u : 2 * u + 2, cols], ADD)
            planes = ring.tile([P, 4, CHUNK], BF16, name="zp1", bufs=2)
            for t in range(4):
                nc.vector.scalar_tensor_tensor(planes[:, t, :], pages[4 + t][:, cols], 1.0, summed[:, t, :], ADD, MULT)
            return weave_z(planes, slice(0, CHUNK), CHUNK)

        def score(c, woven):
            h, cc = divmod(c, 2)
            if cc == 0:
                zq0[h] = quantise(z0_woven[h][:], HALF, f"zq0{h}")
            zq1 = quantise(woven[:], CHUNK, f"zq1{c}")
            banks = []
            for u in range(2):
                y = psum.tile([P, 2, CHUNK], F32, name="y")
                steps = [(a, e, g) for a in range(2) for e in range(2) for g in range(2)]
                for n_step, (a, e, g) in enumerate(steps):
                    i = 2 * u + e
                    codes, scales = zq0[h] if a == 0 else zq1
                    first = (CHUNK * cc if a == 0 else 0) + P * g
                    nc.tensor.matmul_mx(
                        out=y[:, e, P * g : P * g + P],
                        lhsT=w4w[:, a, 2 * P * i : 2 * P * i + 2 * P].bitcast(FP4X4),
                        lhsT_scale=w4s[:, a, P * i : P * i + P],
                        rhs=codes[:, first : first + P].bitcast(FP8X4), rhs_scale=scales[:, first : first + P],
                        start=(n_step == 0), stop=(n_step == len(steps) - 1),
                    )
                neg_sin = ring.tile([P, 2, CHUNK], F32, name="f32row", bufs=16)
                nc.scalar.activation(neg_sin[:], y[:], SIN, scale=-1.0)
                banks.append((y, neg_sin))
            return banks

        def finish(c, banks):
            cols = slice(CHUNK * c, CHUNK * c + CHUNK)
            for u, (y, neg_sin) in enumerate(banks):
                res = ring.tile([P, 2, CHUNK], F32, name="f32row", bufs=16)
                for e in range(2):
                    i = 2 * u + e
                    nc.vector.scalar_tensor_tensor(res[:, e, :], neg_sin[:, e, :], amp[:, i : i + 1], y[:, e, :], MULT, ADD)
                nc.sync.dma_start(out_view[:, 2 * u : 2 * u + 2, cols], res[:])

        chunks = S // CHUNK
        woven_z, scored = {}, {}
        for step in range(chunks + 2):
            if step < chunks:
                woven_z[step] = make_z(step)
            if 0 <= step - 1 < chunks:
                scored[step - 1] = score(step - 1, woven_z[step - 1])
            if 0 <= step - 2 < chunks:
                finish(step - 2, scored[step - 2])
